import numpy as np
import ml_dtypes


def mxq(x, axis, fmt="e4m3"):
    dtype, down = {"e4m3": (ml_dtypes.float8_e4m3fn, 7), "e5m2": (ml_dtypes.float8_e5m2, 14)}[fmt]
    v = np.moveaxis(np.asarray(x, np.float32).astype(ml_dtypes.bfloat16).astype(np.float64), axis, -1)
    blocks = v.reshape(v.shape[:-1] + (-1, 32))
    amax = np.abs(blocks).max(-1, keepdims=True)
    byte = np.maximum(np.where(amax > 0, np.frexp(amax)[1] - 1 + 127, 0) - down, 1)
    scale = np.exp2(byte - 127.0)
    codes = (blocks / scale).astype(np.float32).astype(dtype).astype(np.float64)
    return np.moveaxis((codes * scale).reshape(v.shape), -1, axis)


WIDE = False


def mx_kscale(k):
    if not WIDE:
        return np.ones(k)
    levels = np.array([10, -10, 5, -5, 0])
    if k % 512:
        return np.exp2(np.random.permutation(np.resize(levels, k // 32))).repeat(32)
    a = np.empty((k // 512, 16))
    for p in range(k // 512):
        a[p, :8] = np.random.permutation(np.resize(levels, 8))
        for g in range(8):
            far = levels[np.abs(levels - a[p, g]) >= 10]
            a[p, g + 8] = far[np.random.randint(len(far))]
    return np.exp2(a.ravel()).repeat(32)


def f64(x):
    return np.asarray(x).astype(np.float64)


def striped8(idx):
    return np.asarray(idx).reshape(8, -1, 16).transpose(0, 2, 1).reshape(128, -1).astype(np.uint16)


def unstriped8(offs):
    return offs.reshape(8, 16, -1).transpose(0, 2, 1).reshape(8, -1).astype(np.int64)


def pick8(x, idx, run):
    r = np.arange(len(x))
    return x[r[:, None], idx[r % (8 * run) // run]]


E2M1 = np.array([0.0, 0.5, 1.0, 1.5, 2.0, 3.0, 4.0, 6.0, -0.0, -0.5, -1.0, -1.5, -2.0, -3.0, -4.0, -6.0])


def pack_weight(w, fmt):
    k, n = w.shape
    w = f64(np.asarray(w, np.float32).astype(ml_dtypes.bfloat16)).reshape(k // 32, 32, n)
    amax = np.abs(w).max(1)
    if fmt == "e4m3":
        byte = np.frexp(amax)[1] - 1 + 127 - 7
    else:
        mant, ex = np.frexp(amax / 6.0)
        byte = np.where(mant > 0.5, ex, ex - 1) + 127
    byte = np.clip(np.where(amax > 0, byte, 1), 1, 254)
    scaled = (w * np.exp2(127.0 - byte)[:, None, :]).reshape(k, n).astype(np.float32)
    by_word = np.ascontiguousarray(scaled.reshape(k // 512, 128, 4, n).transpose(0, 1, 3, 2))
    if fmt == "e4m3":
        words = by_word.astype(ml_dtypes.float8_e4m3fn).view(np.uint8)
    else:
        c = by_word.astype(ml_dtypes.float4_e2m1fn).view(np.uint8) & 0xF
        words = (c[..., 0::2] | (c[..., 1::2] << 4)).reshape(k // 512, 128, 2 * n)
    return np.ascontiguousarray(words), np.ascontiguousarray(byte.astype(np.uint8).reshape(k // 512, 16, n))


def unpack_weight(words, scales, fmt):
    g, _, n = scales.shape
    words = np.ascontiguousarray(words).reshape(g, 128, n, -1)
    if fmt == "e4m3":
        vals = words.view(ml_dtypes.float8_e4m3fn).astype(np.float64)
    else:
        nib = np.empty((g, 128, n, 4), np.uint8)
        nib[..., 0::2] = words & 0xF
        nib[..., 1::2] = words >> 4
        vals = E2M1[nib]
    vals = vals * np.repeat(np.exp2(scales.astype(np.float64) - 127.0), 8, axis=1)[..., None]
    return vals.transpose(0, 1, 3, 2).reshape(g * 512, n)


def sigmoid(v):
    return 1.0 / (1.0 + np.exp(-v))


D, T, I, Q = 512, 1024, 512, 128


def setup_inputs():
    n = np.random.standard_normal
    idx = np.stack([np.random.permutation(T)[:I] for _ in range(8)])
    idx2 = np.stack([np.random.permutation(T)[:I] for _ in range(8)])
    idx3 = np.stack([np.random.permutation(T)[:I] for _ in range(8)])
    idx4 = np.stack([np.random.permutation(T)[:I] for _ in range(8)])
    fd = mx_kscale(D)
    keysp = pack_weight(n((D, T)) / fd[:, None], "e2m1")
    return {
        "query": (n((D, Q)) * 1.2 / np.sqrt(D) * fd[:, None]).astype(np.float32),
        "keys_words": keysp[0],
        "keys_scales": keysp[1],
        "lam": (np.random.uniform(0.5, 1.5, (Q, 1))).astype(np.float32),
        "old": (1.0 * n((Q, T))).astype(np.float32),
        "share2": (np.random.uniform(0.4, 1.2, (Q, 1))).astype(np.float32),
        "offs": striped8(idx),
        "offs2": striped8(idx2),
        "offs3": striped8(idx3),
        "offs4": striped8(idx4),
    }


def reference(query, keys_words, keys_scales, lam, old, share2, offs, offs2, offs3, offs4):
    idx = unstriped8(offs)
    idx2 = unstriped8(offs2)
    idx3 = unstriped8(offs3)
    idx4 = unstriped8(offs4)
    keysu = unpack_weight(keys_words, keys_scales, "e2m1")
    queryq = mxq(f64(query), 0, "e4m3")
    a = queryq.T @ keysu
    g1 = sigmoid(pick8(a, idx2, 16) * 2.0)
    w = (pick8(a, idx, 16) * g1 + pick8(a, idx3, 16) * (1.0 - g1)) * f64(lam)
    f1 = np.zeros((Q, T))
    f1[np.arange(Q)[:, None], idx[np.arange(Q) % 128 // 16]] = w
    f2 = np.zeros((Q, T))
    f2[np.arange(Q)[:, None], idx4[np.arange(Q) % 128 // 16]] = w
    y = f64(old) + f1 + f2 * f64(share2)
    return y

@@ -1,0 +1,159 @@
+from contextlib import ExitStack
+
+import concourse.mybir as mybir
+from concourse.masks import make_identity
+
+D, T, I, Q = 512, 1024, 512, 128
+FLOPS = 2 * D * T * Q
+
+F32 = mybir.dt.float32
+BF16 = mybir.dt.bfloat16
+I32 = mybir.dt.int32
+U32 = mybir.dt.uint32
+U16 = mybir.dt.uint16
+U8 = mybir.dt.uint8
+FP8X4 = mybir.dt.float8_e4m3fn_x4
+FP4X4 = mybir.dt.float4_e2m1fn_x4
+ALU = mybir.AluOpType
+ACT = mybir.ActivationFunctionType
+
+P = 128
+PACK = 4
+BANK = 512
+SCORE_COLS = ((0, 128), (128, 384), (384, 640), (640, 896), (896, 1024))
+HALF = I // 2
+STORE_N = 256
+
+
+def tile_attend_conditioned_lean_twiceput_heads_kernel(
+    tc, query, keys_words, keys_scales, lam, old, share2, offs, offs2, offs3, offs4, out
+):
+    nc = tc.nc
+    with ExitStack() as ctx:
+        sb = ctx.enter_context(tc.tile_pool(name="sb", bufs=1))
+        ps = ctx.enter_context(tc.psum_pool(name="ps", bufs=1))
+
+        q_raw = sb.tile([P, PACK, Q], F32, name="q_raw")
+        k_words = sb.tile([P, 2 * T], U8, name="k_words", align_bytes=64)
+        k_scales = sb.tile([P, T], U8, name="k_scales", align_bytes=64)
+        first = sb.tile([P, I // 16], U16, name="first")
+        judge = sb.tile([P, I // 16], U16, name="judge")
+        second = sb.tile([P, I // 16], U16, name="second")
+        other = sb.tile([P, I // 16], U16, name="other")
+        lam_col = sb.tile([P, 1], F32, name="lam_col")
+        share_col = sb.tile([P, 1], F32, name="share_col")
+        old_sb = sb.tile([P, T], F32, name="old_sb")
+        f1 = sb.tile([P, T], F32, name="f1")
+        f2 = sb.tile([P, T], F32, name="f2")
+        ident = sb.tile([P, P], F32, name="ident")
+
+        nc.vector.memset(k_scales[:].bitcast(I32), 0)
+        nc.sync.dma_start(out=q_raw[:], in_=query.rearrange("(p j) q -> p j q", j=PACK))
+        nc.sync.dma_start(out=k_words[:].bitcast(I32), in_=keys_words[0].bitcast(I32))
+        for quad in range(4):
+            nc.sync.dma_start(
+                out=k_scales[32 * quad : 32 * quad + 4, :].bitcast(I32),
+                in_=keys_scales[0, 4 * quad : 4 * quad + 4, :].bitcast(I32),
+            )
+        nc.sync.dma_start(judge[:], offs2)
+        nc.sync.dma_start(first[:], offs)
+        nc.sync.dma_start(second[:], offs3)
+        nc.sync.dma_start(out=lam_col[:], in_=lam)
+        nc.sync.dma_start(out=old_sb[:], in_=old)
+        nc.sync.dma_start(other[:], offs4)
+        nc.sync.dma_start(out=share_col[:], in_=share2)
+        nc.vector.memset(f1[:], 0.0)
+        nc.vector.memset(f2[:], 0.0)
+        make_identity(nc, ident[:])
+
+        q_bf = sb.tile([P, Q, PACK], BF16, name="q_bf", align_bytes=64)
+        q_codes = sb.tile([P, Q], U32, name="q_codes", align_bytes=64)
+        q_scales = sb.tile([P, Q], U8, name="q_scales", align_bytes=64)
+        nc.vector.tensor_copy(out=q_bf[:], in_=q_raw[:].rearrange("p j q -> p q j"))
+        nc.vector.quantize_mx(
+            out=q_codes[:].bitcast(FP8X4), scales=q_scales[:], in_=q_bf[:].rearrange("p q j -> p (q j)")
+        )
+
+        a = sb.tile([P, T], F32, name="a")
+        for c, (lo, hi) in enumerate(SCORE_COLS):
+            cols = slice(lo, hi)
+            acc = ps.tile([P, hi - lo], F32, name="acc%d" % c, tag="bank%d" % c)
+            nc.tensor.matmul_mx(
+                out=acc[:],
+                lhsT=q_codes[:].bitcast(FP8X4),
+                lhsT_scale=q_scales[:],
+                rhs=k_words[:, 2 * cols.start : 2 * cols.stop].bitcast(FP4X4),
+                rhs_scale=k_scales[:, cols],
+                start=True,
+                stop=True,
+            )
+            nc.vector.tensor_copy(out=a[:, cols], in_=acc[:])
+
+        turned = [ps.tile([P, BANK], F32, name="turned%d" % b) for b in range(T // BANK)]
+        for b in range(T // BANK):
+            for j in range(BANK // P):
+                nc.tensor.matmul(
+                    turned[b][:, j * P : (j + 1) * P],
+                    old_sb[:, b * BANK + j * P : b * BANK + (j + 1) * P],
+                    ident[:],
+                    start=(j == 0),
+                    stop=False,
+                    is_transpose=True,
+                )
+
+        gate = sb.tile([P, I], F32, name="gate")
+        rest = sb.tile([P, I], F32, name="rest")
+        a_first = sb.tile([P, I], F32, name="a_first")
+        a_second = sb.tile([P, I], F32, name="a_second")
+        w_first = sb.tile([P, I], F32, name="w_first")
+        w_second = sb.tile([P, I], F32, name="w_second")
+        for h in range(2):
+            s = slice(h * HALF, (h + 1) * HALF)
+            o = slice(h * HALF // 16, (h + 1) * HALF // 16)
+            nc.scalar.activation(gate[:, s], a[:].indirect(judge[:, o]), ACT.Sigmoid, scale=2.0)
+            if h == 0:
+                nc.vector.tensor_copy(a_first[:, s], a[:].indirect(first[:, o]))
+                nc.vector.tensor_copy(a_second[:, s], a[:].indirect(second[:, o]))
+                nc.vector.tensor_scalar(rest[:, s], gate[:, s], -1.0, 1.0, ALU.mult, ALU.add)
+            else:
+                nc.scalar.activation(a_first[:, s], a[:].indirect(first[:, o]), ACT.Copy)
+                nc.scalar.activation(rest[:, s], gate[:, s], ACT.Copy, scale=-1.0, bias=1.0)
+                nc.scalar.activation(a_second[:, s], a[:].indirect(second[:, o]), ACT.Copy)
+            nc.vector.scalar_tensor_tensor(w_first[:, s], a_first[:, s], lam_col[:], gate[:, s], ALU.mult, ALU.mult)
+            nc.vector.scalar_tensor_tensor(w_second[:, s], a_second[:, s], lam_col[:], rest[:, s], ALU.mult, ALU.mult)
+            nc.vector.tensor_tensor(f1[:].indirect(first[:, o]), w_first[:, s], w_second[:, s], ALU.add)
+        nc.vector.tensor_tensor(f2[:].indirect(other[:]), w_first[:], w_second[:], ALU.add)
+
+        sum_t = sb.tile([P, T], F32, name="sum_t")
+        back = [ps.tile([P, BANK], F32, name="back%d" % b, tag="bank%d" % b) for b in range(T // BANK)]
+        for b in range(T // BANK):
+            for j in range(BANK // P):
+                nc.tensor.matmul(
+                    turned[b][:, j * P : (j + 1) * P],
+                    f1[:, b * BANK + j * P : b * BANK + (j + 1) * P],
+                    ident[:],
+                    start=False,
+                    stop=(j == BANK // P - 1),
+                    is_transpose=True,
+                )
+            nc.scalar.copy(out=sum_t[:, b * BANK : (b + 1) * BANK], in_=turned[b][:])
+        for b in range(T // BANK):
+            for j in range(BANK // P):
+                nc.tensor.transpose(
+                    back[b][:, j * P : (j + 1) * P], sum_t[:, b * BANK + j * P : b * BANK + (j + 1) * P], ident[:]
+                )
+
+        result = sb.tile([P, T], F32, name="result")
+        for c in range(T // STORE_N):
+            cols = slice(c * STORE_N, (c + 1) * STORE_N)
+            b = cols.start // BANK
+            nc.vector.scalar_tensor_tensor(
+                result[:, cols],
+                f2[:, cols],
+                share_col[:],
+                back[b][:, cols.start - b * BANK : cols.stop - b * BANK],
+                ALU.mult,
+                ALU.add,
+            )
+            queue = nc.sync if c % 2 == 0 else nc.scalar
+            queue.dma_start(out=out[:, cols], in_=result[:, cols])

@@ -19,10 +19,11 @@ ACT = mybir.ActivationFunctionType
 
 P = 128
 PACK = 4
-BANK = 512
+BANK = 256
 SCORE_COLS = ((0, 128), (128, 384), (384, 640), (640, 896), (896, 1024))
+WORD_COLS = ((0, 384), (384, 1024))
 HALF = I // 2
-STORE_N = 256
+STORE_COLS = ((0, 256), (256, 512), (512, 768), (768, 896), (896, 1024))
 
 
 def tile_attend_conditioned_lean_twiceput_heads_kernel(
@@ -34,7 +35,9 @@ def tile_attend_conditioned_lean_twiceput_heads_kernel(
         ps = ctx.enter_context(tc.psum_pool(name="ps", bufs=1))
 
         q_raw = sb.tile([P, PACK, Q], F32, name="q_raw")
-        k_words = sb.tile([P, 2 * T], U8, name="k_words", align_bytes=64)
+        k_words = [
+            sb.tile([P, 2 * (hi - lo)], U8, name="k_words%d" % n, align_bytes=64) for n, (lo, hi) in enumerate(WORD_COLS)
+        ]
         k_scales = sb.tile([P, T], U8, name="k_scales", align_bytes=64)
         first = sb.tile([P, I // 16], U16, name="first")
         judge = sb.tile([P, I // 16], U16, name="judge")
@@ -49,21 +52,22 @@ def tile_attend_conditioned_lean_twiceput_heads_kernel(
 
         nc.vector.memset(k_scales[:].bitcast(I32), 0)
         nc.sync.dma_start(out=q_raw[:], in_=query.rearrange("(p j) q -> p j q", j=PACK))
-        nc.sync.dma_start(out=k_words[:].bitcast(I32), in_=keys_words[0].bitcast(I32))
+        nc.sync.dma_start(out=k_words[0][:].bitcast(I32), in_=keys_words[0, :, 0 : 2 * WORD_COLS[0][1]].bitcast(I32))
+        nc.sync.dma_start(judge[:], offs2)
         for quad in range(4):
             nc.sync.dma_start(
                 out=k_scales[32 * quad : 32 * quad + 4, :].bitcast(I32),
                 in_=keys_scales[0, 4 * quad : 4 * quad + 4, :].bitcast(I32),
             )
-        nc.sync.dma_start(judge[:], offs2)
+        nc.sync.dma_start(out=k_words[1][:].bitcast(I32), in_=keys_words[0, :, 2 * WORD_COLS[1][0] :].bitcast(I32))
         nc.sync.dma_start(first[:], offs)
         nc.sync.dma_start(second[:], offs3)
         nc.sync.dma_start(out=lam_col[:], in_=lam)
         nc.sync.dma_start(out=old_sb[:], in_=old)
         nc.sync.dma_start(other[:], offs4)
         nc.sync.dma_start(out=share_col[:], in_=share2)
-        nc.vector.memset(f1[:], 0.0)
-        nc.vector.memset(f2[:], 0.0)
+        nc.vector.memset(f1[:].bitcast(I32), 0)
+        nc.vector.memset(f2[:].bitcast(I32), 0)
         make_identity(nc, ident[:])
 
         q_bf = sb.tile([P, Q, PACK], BF16, name="q_bf", align_bytes=64)
@@ -77,19 +81,20 @@ def tile_attend_conditioned_lean_twiceput_heads_kernel(
         a = sb.tile([P, T], F32, name="a")
         for c, (lo, hi) in enumerate(SCORE_COLS):
             cols = slice(lo, hi)
+            part = 0 if hi <= WORD_COLS[0][1] else 1
             acc = ps.tile([P, hi - lo], F32, name="acc%d" % c, tag="bank%d" % c)
             nc.tensor.matmul_mx(
                 out=acc[:],
                 lhsT=q_codes[:].bitcast(FP8X4),
                 lhsT_scale=q_scales[:],
-                rhs=k_words[:, 2 * cols.start : 2 * cols.stop].bitcast(FP4X4),
+                rhs=k_words[part][:, 2 * (lo - WORD_COLS[part][0]) : 2 * (hi - WORD_COLS[part][0])].bitcast(FP4X4),
                 rhs_scale=k_scales[:, cols],
                 start=True,
                 stop=True,
             )
             nc.vector.tensor_copy(out=a[:, cols], in_=acc[:])
 
-        turned = [ps.tile([P, BANK], F32, name="turned%d" % b) for b in range(T // BANK)]
+        turned = [ps.tile([P, BANK], F32, name="turned%d" % b, tag="bank%d" % b) for b in range(T // BANK)]
         for b in range(T // BANK):
             for j in range(BANK // P):
                 nc.tensor.matmul(
@@ -125,7 +130,7 @@ def tile_attend_conditioned_lean_twiceput_heads_kernel(
         nc.vector.tensor_tensor(f2[:].indirect(other[:]), w_first[:], w_second[:], ALU.add)
 
         sum_t = sb.tile([P, T], F32, name="sum_t")
-        back = [ps.tile([P, BANK], F32, name="back%d" % b, tag="bank%d" % b) for b in range(T // BANK)]
+        back = [ps.tile([P, BANK], F32, name="back%d" % b, tag="bank%d" % (4 + b)) for b in range(T // BANK)]
         for b in range(T // BANK):
             for j in range(BANK // P):
                 nc.tensor.matmul(
@@ -144,8 +149,8 @@ def tile_attend_conditioned_lean_twiceput_heads_kernel(
                 )
 
         result = sb.tile([P, T], F32, name="result")
-        for c in range(T // STORE_N):
-            cols = slice(c * STORE_N, (c + 1) * STORE_N)
+        for c, (lo, hi) in enumerate(STORE_COLS):
+            cols = slice(lo, hi)
             b = cols.start // BANK
             nc.vector.scalar_tensor_tensor(
                 result[:, cols],

from contextlib import ExitStack

import concourse.mybir as mybir
from concourse.masks import make_identity

D, T, I, Q = 512, 1024, 512, 128
FLOPS = 2 * D * T * Q

F32 = mybir.dt.float32
BF16 = mybir.dt.bfloat16
I32 = mybir.dt.int32
U32 = mybir.dt.uint32
U16 = mybir.dt.uint16
U8 = mybir.dt.uint8
FP8X4 = mybir.dt.float8_e4m3fn_x4
FP4X4 = mybir.dt.float4_e2m1fn_x4
ALU = mybir.AluOpType
ACT = mybir.ActivationFunctionType

P = 128
PACK = 4
BANK = 256
SCORE_COLS = ((0, 128), (128, 384), (384, 640), (640, 896), (896, 1024))
WORD_COLS = ((0, 384), (384, 1024))
HALF = I // 2
STORE_COLS = ((0, 256), (256, 512), (512, 768), (768, 896), (896, 1024))


def tile_attend_conditioned_lean_twiceput_heads_kernel(
    tc, query, keys_words, keys_scales, lam, old, share2, offs, offs2, offs3, offs4, out
):
    nc = tc.nc
    with ExitStack() as ctx:
        sb = ctx.enter_context(tc.tile_pool(name="sb", bufs=1))
        ps = ctx.enter_context(tc.psum_pool(name="ps", bufs=1))

        q_raw = sb.tile([P, PACK, Q], F32, name="q_raw")
        k_words = [
            sb.tile([P, 2 * (hi - lo)], U8, name="k_words%d" % n, align_bytes=64) for n, (lo, hi) in enumerate(WORD_COLS)
        ]
        k_scales = sb.tile([P, T], U8, name="k_scales", align_bytes=64)
        first = sb.tile([P, I // 16], U16, name="first")
        judge = sb.tile([P, I // 16], U16, name="judge")
        second = sb.tile([P, I // 16], U16, name="second")
        other = sb.tile([P, I // 16], U16, name="other")
        lam_col = sb.tile([P, 1], F32, name="lam_col")
        share_col = sb.tile([P, 1], F32, name="share_col")
        old_sb = sb.tile([P, T], F32, name="old_sb")
        f1 = sb.tile([P, T], F32, name="f1")
        f2 = sb.tile([P, T], F32, name="f2")
        ident = sb.tile([P, P], F32, name="ident")

        nc.vector.memset(k_scales[:].bitcast(I32), 0)
        nc.sync.dma_start(out=q_raw[:], in_=query.rearrange("(p j) q -> p j q", j=PACK))
        nc.sync.dma_start(out=k_words[0][:].bitcast(I32), in_=keys_words[0, :, 0 : 2 * WORD_COLS[0][1]].bitcast(I32))
        nc.sync.dma_start(judge[:], offs2)
        for quad in range(4):
            nc.sync.dma_start(
                out=k_scales[32 * quad : 32 * quad + 4, :].bitcast(I32),
                in_=keys_scales[0, 4 * quad : 4 * quad + 4, :].bitcast(I32),
            )
        nc.sync.dma_start(out=k_words[1][:].bitcast(I32), in_=keys_words[0, :, 2 * WORD_COLS[1][0] :].bitcast(I32))
        nc.sync.dma_start(first[:], offs)
        nc.sync.dma_start(second[:], offs3)
        nc.sync.dma_start(out=lam_col[:], in_=lam)
        nc.sync.dma_start(out=old_sb[:], in_=old)
        nc.sync.dma_start(other[:], offs4)
        nc.sync.dma_start(out=share_col[:], in_=share2)
        nc.vector.memset(f1[:].bitcast(I32), 0)
        nc.vector.memset(f2[:].bitcast(I32), 0)
        make_identity(nc, ident[:])

        q_bf = sb.tile([P, Q, PACK], BF16, name="q_bf", align_bytes=64)
        q_codes = sb.tile([P, Q], U32, name="q_codes", align_bytes=64)
        q_scales = sb.tile([P, Q], U8, name="q_scales", align_bytes=64)
        nc.vector.tensor_copy(out=q_bf[:], in_=q_raw[:].rearrange("p j q -> p q j"))
        nc.vector.quantize_mx(
            out=q_codes[:].bitcast(FP8X4), scales=q_scales[:], in_=q_bf[:].rearrange("p q j -> p (q j)")
        )

        a = sb.tile([P, T], F32, name="a")
        for c, (lo, hi) in enumerate(SCORE_COLS):
            cols = slice(lo, hi)
            part = 0 if hi <= WORD_COLS[0][1] else 1
            acc = ps.tile([P, hi - lo], F32, name="acc%d" % c, tag="bank%d" % c)
            nc.tensor.matmul_mx(
                out=acc[:],
                lhsT=q_codes[:].bitcast(FP8X4),
                lhsT_scale=q_scales[:],
                rhs=k_words[part][:, 2 * (lo - WORD_COLS[part][0]) : 2 * (hi - WORD_COLS[part][0])].bitcast(FP4X4),
                rhs_scale=k_scales[:, cols],
                start=True,
                stop=True,
            )
            nc.vector.tensor_copy(out=a[:, cols], in_=acc[:])

        turned = [ps.tile([P, BANK], F32, name="turned%d" % b, tag="bank%d" % b) for b in range(T // BANK)]
        for b in range(T // BANK):
            for j in range(BANK // P):
                nc.tensor.matmul(
                    turned[b][:, j * P : (j + 1) * P],
                    old_sb[:, b * BANK + j * P : b * BANK + (j + 1) * P],
                    ident[:],
                    start=(j == 0),
                    stop=False,
                    is_transpose=True,
                )

        gate = sb.tile([P, I], F32, name="gate")
        rest = sb.tile([P, I], F32, name="rest")
        a_first = sb.tile([P, I], F32, name="a_first")
        a_second = sb.tile([P, I], F32, name="a_second")
        w_first = sb.tile([P, I], F32, name="w_first")
        w_second = sb.tile([P, I], F32, name="w_second")
        for h in range(2):
            s = slice(h * HALF, (h + 1) * HALF)
            o = slice(h * HALF // 16, (h + 1) * HALF // 16)
            nc.scalar.activation(gate[:, s], a[:].indirect(judge[:, o]), ACT.Sigmoid, scale=2.0)
            if h == 0:
                nc.vector.tensor_copy(a_first[:, s], a[:].indirect(first[:, o]))
                nc.vector.tensor_copy(a_second[:, s], a[:].indirect(second[:, o]))
                nc.vector.tensor_scalar(rest[:, s], gate[:, s], -1.0, 1.0, ALU.mult, ALU.add)
            else:
                nc.scalar.activation(a_first[:, s], a[:].indirect(first[:, o]), ACT.Copy)
                nc.scalar.activation(rest[:, s], gate[:, s], ACT.Copy, scale=-1.0, bias=1.0)
                nc.scalar.activation(a_second[:, s], a[:].indirect(second[:, o]), ACT.Copy)
            nc.vector.scalar_tensor_tensor(w_first[:, s], a_first[:, s], lam_col[:], gate[:, s], ALU.mult, ALU.mult)
            nc.vector.scalar_tensor_tensor(w_second[:, s], a_second[:, s], lam_col[:], rest[:, s], ALU.mult, ALU.mult)
            nc.vector.tensor_tensor(f1[:].indirect(first[:, o]), w_first[:, s], w_second[:, s], ALU.add)
        nc.vector.tensor_tensor(f2[:].indirect(other[:]), w_first[:], w_second[:], ALU.add)

        sum_t = sb.tile([P, T], F32, name="sum_t")
        back = [ps.tile([P, BANK], F32, name="back%d" % b, tag="bank%d" % (4 + b)) for b in range(T // BANK)]
        for b in range(T // BANK):
            for j in range(BANK // P):
                nc.tensor.matmul(
                    turned[b][:, j * P : (j + 1) * P],
                    f1[:, b * BANK + j * P : b * BANK + (j + 1) * P],
                    ident[:],
                    start=False,
                    stop=(j == BANK // P - 1),
                    is_transpose=True,
                )
            nc.scalar.copy(out=sum_t[:, b * BANK : (b + 1) * BANK], in_=turned[b][:])
        for b in range(T // BANK):
            for j in range(BANK // P):
                nc.tensor.transpose(
                    back[b][:, j * P : (j + 1) * P], sum_t[:, b * BANK + j * P : b * BANK + (j + 1) * P], ident[:]
                )

        result = sb.tile([P, T], F32, name="result")
        for c, (lo, hi) in enumerate(STORE_COLS):
            cols = slice(lo, hi)
            b = cols.start // BANK
            nc.vector.scalar_tensor_tensor(
                result[:, cols],
                f2[:, cols],
                share_col[:],
                back[b][:, cols.start - b * BANK : cols.stop - b * BANK],
                ALU.mult,
                ALU.add,
            )
            queue = nc.sync if c % 2 == 0 else nc.scalar
            queue.dma_start(out=out[:, cols], in_=result[:, cols])
